import numpy as np
import ml_dtypes


def mxq(x, axis, fmt="e4m3"):
    dtype, down = {"e4m3": (ml_dtypes.float8_e4m3fn, 7), "e5m2": (ml_dtypes.float8_e5m2, 14)}[fmt]
    v = np.moveaxis(np.asarray(x, np.float32).astype(ml_dtypes.bfloat16).astype(np.float64), axis, -1)
    blocks = v.reshape(v.shape[:-1] + (-1, 32))
    amax = np.abs(blocks).max(-1, keepdims=True)
    byte = np.maximum(np.where(amax > 0, np.frexp(amax)[1] - 1 + 127, 0) - down, 1)
    scale = np.exp2(byte - 127.0)
    codes = (blocks / scale).astype(np.float32).astype(dtype).astype(np.float64)
    return np.moveaxis((codes * scale).reshape(v.shape), -1, axis)


WIDE = False


def mx_kscale(k):
    if not WIDE:
        return np.ones(k)
    levels = np.array([10, -10, 5, -5, 0])
    if k % 512:
        return np.exp2(np.random.permutation(np.resize(levels, k // 32))).repeat(32)
    a = np.empty((k // 512, 16))
    for p in range(k // 512):
        a[p, :8] = np.random.permutation(np.resize(levels, 8))
        for g in range(8):
            far = levels[np.abs(levels - a[p, g]) >= 10]
            a[p, g + 8] = far[np.random.randint(len(far))]
    return np.exp2(a.ravel()).repeat(32)


def f64(x):
    return np.asarray(x).astype(np.float64)


def striped(idx):
    return np.tile(idx.reshape(-1, 16).T, (8, 1)).astype(np.uint16)


def unstriped(offs):
    return offs[:16].T.reshape(-1).astype(np.int64)


E2M1 = np.array([0.0, 0.5, 1.0, 1.5, 2.0, 3.0, 4.0, 6.0, -0.0, -0.5, -1.0, -1.5, -2.0, -3.0, -4.0, -6.0])


def pack_weight(w, fmt):
    k, n = w.shape
    w = f64(np.asarray(w, np.float32).astype(ml_dtypes.bfloat16)).reshape(k // 32, 32, n)
    amax = np.abs(w).max(1)
    if fmt == "e4m3":
        byte = np.frexp(amax)[1] - 1 + 127 - 7
    else:
        mant, ex = np.frexp(amax / 6.0)
        byte = np.where(mant > 0.5, ex, ex - 1) + 127
    byte = np.clip(np.where(amax > 0, byte, 1), 1, 254)
    scaled = (w * np.exp2(127.0 - byte)[:, None, :]).reshape(k, n).astype(np.float32)
    by_word = np.ascontiguousarray(scaled.reshape(k // 512, 128, 4, n).transpose(0, 1, 3, 2))
    if fmt == "e4m3":
        words = by_word.astype(ml_dtypes.float8_e4m3fn).view(np.uint8)
    else:
        c = by_word.astype(ml_dtypes.float4_e2m1fn).view(np.uint8) & 0xF
        words = (c[..., 0::2] | (c[..., 1::2] << 4)).reshape(k // 512, 128, 2 * n)
    return np.ascontiguousarray(words), np.ascontiguousarray(byte.astype(np.uint8).reshape(k // 512, 16, n))


def unpack_weight(words, scales, fmt):
    g, _, n = scales.shape
    words = np.ascontiguousarray(words).reshape(g, 128, n, -1)
    if fmt == "e4m3":
        vals = words.view(ml_dtypes.float8_e4m3fn).astype(np.float64)
    else:
        nib = np.empty((g, 128, n, 4), np.uint8)
        nib[..., 0::2] = words & 0xF
        nib[..., 1::2] = words >> 4
        vals = E2M1[nib]
    vals = vals * np.repeat(np.exp2(scales.astype(np.float64) - 127.0), 8, axis=1)[..., None]
    return vals.transpose(0, 1, 3, 2).reshape(g * 512, n)


def gelu(v):
    return 0.5 * v * (1.0 + np.tanh(np.sqrt(2.0 / np.pi) * (v + 0.044715 * v**3)))


K, K2, T, S, H, N, T2, P = 1024, 512, 2048, 512, 1024, 512, 2048, 1024

def setup_inputs():
    n = np.random.standard_normal
    s, s2, u = mx_kscale(K)[:, None], mx_kscale(K2)[:, None], mx_kscale(H)[:, None]
    d = {}
    d["tab_words"], d["tab_scales"] = pack_weight(n((K, T)) * s, "e4m3")
    d["tab2_words"], d["tab2_scales"] = pack_weight(n((K2, T)) * s2, "e4m3")
    d["offs"] = striped(np.random.permutation(T)[:S])
    d["offs2"] = striped(np.random.permutation(T)[:S])
    perm = np.random.permutation(T2)
    d["offs3"] = striped(perm[:S])
    d["offs4"] = striped(perm[S:2 * S])
    d["offs5"] = striped(np.random.permutation(T2)[:P])
    d["wa_words"], d["wa_scales"] = pack_weight(n((K, H)) / K ** 0.5 / s * u.T, "e2m1")
    d["wb"] = (n((K, H)) / K ** 0.5 / s * u.T).astype(np.float32)
    d["wc_words"], d["wc_scales"] = pack_weight(1.6 * n((K2, H)) / K2 ** 0.5 / s2, "e4m3")
    d["gc"] = (2.2 * n(H) * u[:, 0]).astype(np.float32)
    d["page0"] = (n((H, T2)) * u).astype(np.float32)
    d["wg1"] = np.exp(0.3 * n((128, S))).astype(np.float32)
    d["wg2"] = np.exp(0.3 * n((128, S))).astype(np.float32)
    d["gx"] = np.exp(0.4 * n(H)).astype(np.float32)
    d["w4"] = (n((H, N)) / H ** 0.5 / u).astype(np.float32)
    d["w5_words"], d["w5_scales"] = pack_weight(n((H, N)) / H ** 0.5 / u, "e2m1")
    return d

def reference(tab_words, tab_scales, tab2_words, tab2_scales, offs, offs2, offs3, offs4, offs5, wa_words, wa_scales, wb, wc_words, wc_scales, gc, page0, wg1, wg2, gx, w4, w5_words, w5_scales):
    v = unpack_weight(tab_words, tab_scales, "e4m3")[:, unstriped(offs)]
    v2 = unpack_weight(tab2_words, tab2_scales, "e4m3")[:, unstriped(offs2)]
    a = unpack_weight(wa_words, wa_scales, "e2m1").T @ v
    b = mxq(f64(wb), 0, "e4m3").T @ v
    h1 = np.minimum(a, b)
    c = unpack_weight(wc_words, wc_scales, "e4m3").T @ v2
    h2 = f64(gc)[:, None] * np.exp(-np.abs(c))
    page = f64(page0).copy()
    page[:, unstriped(offs3)] = np.tile(f64(wg1), (H // 128, 1)) * h1
    page[:, unstriped(offs4)] = np.tile(f64(wg2), (H // 128, 1)) * h2
    x = mxq(page[:, unstriped(offs5)] * f64(gx)[:, None], 0, "e4m3")
    y1 = mxq(f64(w4), 0, "e4m3").T @ x
    y2 = unpack_weight(w5_words, w5_scales, "e2m1").T @ x
    return np.maximum(y1, y2)

@@ -1,0 +1,326 @@
+from contextlib import ExitStack
+
+import concourse.mybir as mybir
+
+F32 = mybir.dt.float32
+BF16 = mybir.dt.bfloat16
+I32 = mybir.dt.int32
+U32 = mybir.dt.uint32
+U16 = mybir.dt.uint16
+U8 = mybir.dt.uint8
+FP8X4 = mybir.dt.float8_e4m3fn_x4
+FP4X4 = mybir.dt.float4_e2m1fn_x4
+ACT = mybir.ActivationFunctionType
+ALU = mybir.AluOpType
+
+K, K2, T, S, H, N, T2, PICK = 1024, 512, 2048, 512, 1024, 512, 2048, 1024
+P = 128
+PACK = 4
+PASS = P * PACK
+QUADS = 4
+HALF = PICK // 2
+
+FLOPS = 2 * (2 * K * H * S + K2 * H * S + 2 * H * N * PICK)
+
+
+def tile_list_roast_profile_shelf_kernel(
+    tc, tab_words, tab_scales, tab2_words, tab2_scales, offs, offs2, offs3, offs4, offs5,
+    wa_words, wa_scales, wb, wc_words, wc_scales, gc, page0, wg1, wg2, gx, w4, w5_words, w5_scales, out,
+):
+    nc = tc.nc
+    with ExitStack() as ctx:
+        keep = ctx.enter_context(tc.tile_pool(name="keep", bufs=1))
+        ring = ctx.enter_context(tc.tile_pool(name="ring", bufs=2))
+        psum = ctx.enter_context(tc.psum_pool(name="psum", bufs=1))
+
+        def bank(i):
+            return psum.tile([P, 512], F32, name=f"bank{i}", tag=f"bank{i}")
+
+        def load_list(src, name):
+            tile = keep.tile([P, src.shape[1]], U16, name=name)
+            nc.sync.dma_start(tile[:], src)
+            return tile
+
+        def big(shape, dtype, name):
+            return ring.tile(shape, dtype, name=name, tag="big", bufs=4, align_bytes=64)
+
+        def load_table_words(src, name):
+            tile = big([P, T], I32, name)
+            nc.sync.dma_start(tile[:], src.rearrange("p t i -> p (t i)").bitcast(I32))
+            return tile
+
+        def zeroed(engine, width, name):
+            tile = keep.tile([P, width], U8, name=name, align_bytes=64)
+            engine.memset(tile[:].bitcast(I32), 0)
+            return tile
+
+        def load_plane(queue, tile, src):
+            passes = src.shape[0]
+            for q in range(QUADS):
+                queue.dma_start(
+                    tile[32 * q : 32 * q + 4, :].bitcast(I32).rearrange("r (a c) -> r a c", a=passes),
+                    src[:, 4 * q : 4 * q + 4, :].bitcast(I32).rearrange("a r c -> r a c"),
+                )
+
+        def load_dealt_gain(queue, tile, src, t0, t1):
+            rows = src.rearrange("(q t) s -> q t s", t=PACK)
+            for q in (0, 2, 1, 3):
+                queue.dma_start(tile[32 * q : 32 * q + 32, :, :], rows[:, t0:t1, :])
+
+        page_rows = page0.rearrange("(b p t) c -> b t p c", p=P, t=PACK)
+        pages = {}
+
+        def load_page(b, t):
+            pages[b, t] = keep.tile([P, T2], F32, name=f"page{b}{t}")
+            nc.sync.dma_start(pages[b, t][:], page_rows[b, t])
+
+        def load_float_weight(src, name):
+            tile = big([P, PACK, 512], F32, name)
+            nc.sync.dma_start(tile[:], src.rearrange("(p i) c -> p i c", i=PACK))
+            return tile
+
+        def quantise(src, name):
+            codes = keep.tile([P, 512], U32, name=name + "_codes", align_bytes=64)
+            scales = keep.tile([P, 512], U8, name=name + "_scales", align_bytes=64)
+            nc.vector.quantize_mx(out=codes[:].bitcast(FP8X4), scales=scales[:], in_=src)
+            return codes, scales
+
+        def load_plane_filled(tile, src):
+            for q in range(QUADS):
+                nc.sync.dma_start(
+                    tile[32 * q : 32 * q + 32, :].bitcast(I32),
+                    src[4 * q : 4 * q + 4, :].bitcast(I32).partition_broadcast(8),
+                )
+
+        wa_plane_raw = zeroed(nc.vector, 2 * H, "wa_plane_raw")
+        t_plane = zeroed(nc.vector, T, "t_plane")
+        v_plane1 = zeroed(nc.vector, S, "v_plane1")
+        w5_plane = zeroed(nc.vector, 2 * N, "w5_plane")
+
+        idx2 = load_list(offs2, "idx2")
+        t2_plane = keep.tile([P, T], U8, name="t2_plane", align_bytes=64)
+        load_plane_filled(t2_plane, tab2_scales[0])
+        t2_words = load_table_words(tab2_words[0], "t2_words")
+        wc_raw = ring.tile([P, H], I32, name="wc_raw", tag="wraw", bufs=1, align_bytes=64)
+        nc.sync.dma_start(wc_raw[:], wc_words[0].rearrange("p c i -> p (c i)").bitcast(I32))
+        wc_plane_raw = keep.tile([P, H], U8, name="wc_plane_raw", align_bytes=64)
+        load_plane_filled(wc_plane_raw, wc_scales[0])
+        load_page(0, 0)
+        gc_col = keep.tile([P, 2, PACK], F32, name="gc_col")
+        nc.sync.dma_start(gc_col[:], gc.rearrange("(b p t) -> p b t", p=P, t=PACK))
+        idx4 = load_list(offs4, "idx4")
+        wg2_first = keep.tile([P, 1, S], F32, name="wg2_first")
+        load_dealt_gain(nc.sync, wg2_first, wg2, 0, 1)
+        idx = load_list(offs, "idx")
+        load_plane(nc.gpsimd, wa_plane_raw, wa_scales)
+        for q in range(QUADS):
+            nc.gpsimd.dma_start(
+                t_plane[32 * q : 32 * q + 8, :].bitcast(I32), tab_scales[:, 4 * q : 4 * q + 4, :].bitcast(I32)
+            )
+        load_page(1, 0)
+        wg2_rest = keep.tile([P, PACK - 1, S], F32, name="wg2_rest")
+        load_dealt_gain(nc.sync, wg2_rest, wg2, 1, PACK)
+        load_page(0, 1)
+        t_words = [load_table_words(tab_words[0], "t_words0")]
+        load_page(0, 2)
+        t_words.append(load_table_words(tab_words[1], "t_words1"))
+        load_page(0, 3)
+        wb_raw = {}
+
+        def load_wb(a, b):
+            wb_raw[a, b] = load_float_weight(wb[PASS * a : PASS * (a + 1), 512 * b : 512 * (b + 1)], f"wb_raw{a}{b}")
+
+        load_wb(0, 0)
+        wa_raw = ring.tile([P, H], I32, name="wa_raw", tag="wraw", bufs=1, align_bytes=64)
+        nc.sync.dma_start(
+            wa_raw[:].rearrange("p (a c) -> p a c", a=2), wa_words.bitcast(I32).rearrange("a p c -> p a c")
+        )
+        load_wb(1, 0)
+        load_page(1, 1)
+        wg1_first = keep.tile([P, 1, S], F32, name="wg1_first")
+        load_dealt_gain(nc.sync, wg1_first, wg1, 0, 1)
+        idx3 = load_list(offs3, "idx3")
+        load_page(1, 2)
+        idx5 = load_list(offs5, "idx5")
+        gx_col = keep.tile([P, 2, PACK], F32, name="gx_col")
+        nc.sync.dma_start(gx_col[:], gx.rearrange("(b p t) -> p b t", p=P, t=PACK))
+        wg1_rest = keep.tile([P, PACK - 1, S], F32, name="wg1_rest")
+        load_dealt_gain(nc.sync, wg1_rest, wg1, 1, PACK)
+        load_page(1, 3)
+
+        v2_plane = keep.tile([P, S], U8, name="v2_plane", align_bytes=64)
+        nc.vector.tensor_copy(v2_plane[:], t2_plane[:].indirect(idx2[:]))
+        v2_codes = keep.tile([P, S], U32, name="v2_codes", align_bytes=64)
+        nc.vector.tensor_copy(v2_codes[:], t2_words[:].bitcast(U32).indirect(idx2[:]))
+        wc_plane = keep.tile([P, H], U8, name="wc_plane", align_bytes=64)
+        wc_codes = keep.tile([P, H], U32, name="wc_codes", align_bytes=64)
+        for b in range(2):
+            nc.vector.tensor_copy(
+                wc_plane[:, 512 * b : 512 * (b + 1)].rearrange("p (t m) -> p t m", t=PACK),
+                wc_plane_raw[:, 512 * b : 512 * (b + 1)].rearrange("p (m t) -> p t m", t=PACK),
+            )
+            nc.scalar.copy(
+                wc_codes[:, 512 * b : 512 * (b + 1)].rearrange("p (t m) -> p m t", t=PACK),
+                wc_raw[:, 512 * b : 512 * (b + 1)].bitcast(U32).rearrange("p (m t) -> p m t", t=PACK),
+            )
+
+        def curve(b, t, u):
+            cols = slice(512 * b + P * t, 512 * b + P * (t + 1))
+            c = bank(u % 2)
+            nc.tensor.matmul_mx(
+                out=c[:], lhsT=wc_codes[:, cols].bitcast(FP8X4), lhsT_scale=wc_plane[:, cols],
+                rhs=v2_codes[:].bitcast(FP8X4), rhs_scale=v2_plane[:], start=True, stop=True,
+            )
+            size = ring.tile([P, S], F32, name="size", tag="staged", bufs=2)
+            nc.scalar.activation(size[:], c[:], ACT.Abs)
+            feature = ring.tile([P, S], F32, name="feature", tag="result", bufs=8)
+            nc.scalar.activation(feature[:], size[:], ACT.Exp, scale=-1.0)
+            nc.scalar.activation(feature[:], feature[:], ACT.Copy, scale=gc_col[:, b, t : t + 1])
+            gain = wg2_first[:, 0, :] if t == 0 else wg2_rest[:, t - 1, :]
+            nc.vector.tensor_tensor(pages[b, t][:].indirect(idx4[:]), feature[:], gain, ALU.mult)
+
+        def round_wb(raw, name):
+            rounded = ring.tile([P, 512 * PACK], BF16, name=name, tag="rounded", bufs=4, align_bytes=64)
+            nc.scalar.copy(
+                rounded[:].rearrange("p (t m i) -> p m t i", t=PACK, i=PACK),
+                raw[:].rearrange("p i (m t) -> p m t i", t=PACK),
+            )
+            return rounded
+
+        def round_w4(raw, name):
+            rounded = ring.tile([P, 512 * PACK], BF16, name=name, tag="rounded", bufs=4, align_bytes=64)
+            nc.scalar.copy(rounded[:].rearrange("p (c i) -> p c i", i=PACK), raw[:].rearrange("p i c -> p c i"))
+            return rounded
+
+        wb_q, w4_q, v_codes = {}, {}, {}
+
+        def prepare_wb(a, b):
+            wb_q[a, b] = quantise(round_wb(wb_raw[a, b], f"wb_bf{a}{b}")[:], f"wb{a}{b}")
+
+        def prepare_w4(b):
+            raw = load_float_weight(w4[PASS * b : PASS * (b + 1), :], f"w4_raw{b}")
+            w4_q[b] = quantise(round_w4(raw, f"w4_bf{b}")[:], f"w4{b}")
+
+        def gather_v(a):
+            v_codes[a] = keep.tile([P, S], U32, name=f"v_codes{a}", align_bytes=64)
+            nc.vector.tensor_copy(v_codes[a][:], t_words[a][:].bitcast(U32).indirect(idx[:]))
+
+        curve(0, 0, 0)
+        v_planes = keep.tile([P, S], U8, name="v_planes", align_bytes=64)
+        nc.vector.tensor_copy(v_planes[:], t_plane[:].indirect(idx[:]))
+        for q in range(QUADS):
+            nc.gpsimd.dma_start(
+                v_plane1[32 * q : 32 * q + 4, :].bitcast(I32), v_planes[32 * q + 4 : 32 * q + 8, :].bitcast(I32)
+            )
+        wa_plane = keep.tile([P, 2 * H], U8, name="wa_plane", align_bytes=64)
+        nc.vector.tensor_copy(
+            wa_plane[:].rearrange("p (g t m) -> p g t m", g=4, t=PACK),
+            wa_plane_raw[:].rearrange("p (g m t) -> p g t m", g=4, t=PACK),
+        )
+        curve(1, 0, 1)
+        curve(0, 1, 2)
+        gather_v(0)
+        curve(0, 2, 3)
+        gather_v(1)
+        curve(0, 3, 4)
+        prepare_wb(0, 0)
+        wa_codes = keep.tile([P, 2 * H], U16, name="wa_codes", align_bytes=64)
+        nc.scalar.copy(
+            wa_codes[:].rearrange("p (g t m) -> p g t m", g=4, t=PACK),
+            wa_raw[:].bitcast(U16).rearrange("p (g m t) -> p g t m", g=4, t=PACK),
+        )
+        prepare_wb(1, 0)
+        curve(1, 1, 5)
+        curve(1, 2, 6)
+        curve(1, 3, 7)
+
+        v_scales = (v_planes, v_plane1)
+        x_bf, x_q = {}, {}
+
+        def bean_features(b, t):
+            u = PACK * b + t
+            pa, pb = bank(2 + u % 2), bank(4 + u % 2)
+            for a in range(2):
+                cols = slice(H * a + 512 * b + P * t, H * a + 512 * b + P * (t + 1))
+                nc.tensor.matmul_mx(
+                    out=pa[:], lhsT=wa_codes[:, cols].bitcast(FP4X4), lhsT_scale=wa_plane[:, cols],
+                    rhs=v_codes[a][:].bitcast(FP8X4), rhs_scale=v_scales[a][:], start=a == 0, stop=a == 1,
+                )
+            cols = slice(P * t, P * (t + 1))
+            for a in range(2):
+                codes, scales = wb_q[a, b]
+                nc.tensor.matmul_mx(
+                    out=pb[:], lhsT=codes[:, cols].bitcast(FP8X4), lhsT_scale=scales[:, cols],
+                    rhs=v_codes[a][:].bitcast(FP8X4), rhs_scale=v_scales[a][:], start=a == 0, stop=a == 1,
+                )
+            first = ring.tile([P, S], F32, name="first", tag="staged", bufs=2)
+            nc.scalar.copy(first[:], pa[:])
+            lower = ring.tile([P, S], F32, name="lower", tag="result", bufs=8)
+            nc.vector.tensor_tensor(lower[:], pb[:], first[:], ALU.min)
+            return lower
+
+        def put_bean(b, t, lower):
+            gain = wg1_first[:, 0, :] if t == 0 else wg1_rest[:, t - 1, :]
+            nc.vector.tensor_tensor(pages[b, t][:].indirect(idx3[:]), lower[:], gain, ALU.mult)
+
+        def fetch(b, t, h):
+            if t == 0:
+                x_bf[b, h] = ring.tile([P, HALF, PACK], BF16, name=f"x_bf{b}{h}", tag="x_bf", bufs=4, align_bytes=64)
+            picked = ring.tile([P, HALF], F32, name="picked", tag="picked", bufs=4)
+            w = HALF // 16
+            nc.vector.tensor_copy(picked[:], pages[b, t][:].indirect(idx5[:, w * h : w * (h + 1)]))
+            nc.scalar.activation(x_bf[b, h][:, :, t], picked[:], ACT.Copy, scale=gx_col[:, b, t : t + 1])
+
+        def quantise_x(b, h):
+            x_q[b, h] = quantise(x_bf[b, h][:].rearrange("p c i -> p (c i)"), f"x{b}{h}")
+
+        w5_codes = keep.tile([P, 2 * N], U16, name="w5_codes", align_bytes=64)
+
+        def scores(h):
+            for n in range(N // P):
+                y1, y2 = bank(2 * n), bank(2 * n + 1)
+                cols = slice(P * n, P * (n + 1))
+                for b in range(2):
+                    wide = slice(N * b + P * n, N * b + P * (n + 1))
+                    codes, scales = x_q[b, h]
+                    nc.tensor.matmul_mx(
+                        out=y2[:], lhsT=w5_codes[:, wide].bitcast(FP4X4), lhsT_scale=w5_plane[:, wide],
+                        rhs=codes[:].bitcast(FP8X4), rhs_scale=scales[:], start=b == 0, stop=b == 1,
+                    )
+                    nc.tensor.matmul_mx(
+                        out=y1[:], lhsT=w4_q[b][0][:, cols].bitcast(FP8X4), lhsT_scale=w4_q[b][1][:, cols],
+                        rhs=codes[:].bitcast(FP8X4), rhs_scale=scales[:], start=b == 0, stop=b == 1,
+                    )
+                second = ring.tile([P, HALF], F32, name="second", tag="staged", bufs=2)
+                nc.scalar.copy(second[:], y2[:])
+                larger = ring.tile([P, HALF], F32, name="larger", tag="result", bufs=8)
+                nc.vector.tensor_tensor(larger[:], y1[:], second[:], ALU.max)
+                nc.sync.dma_start(out[cols, HALF * h : HALF * (h + 1)], larger[:])
+
+        order = [(b, t) for b in range(2) for t in range(PACK)]
+        lower = bean_features(0, 0)
+        for u, (b, t) in enumerate(order):
+            put_bean(b, t, lower)
+            if u == 0:
+                for a in range(2):
+                    load_wb(a, 1)
+                    prepare_wb(a, 1)
+            if u == 1:
+                prepare_w4(0)
+                prepare_w4(1)
+                nc.sync.dma_start(
+                    w5_codes[:].bitcast(I32).rearrange("p (a c) -> p a c", a=2),
+                    w5_words.bitcast(I32).rearrange("a p c -> p a c"),
+                )
+                load_plane(nc.sync, w5_plane, w5_scales)
+            if u + 1 < len(order):
+                lower = bean_features(*order[u + 1])
+            if u == PACK:
+                quantise_x(0, 0)
+                quantise_x(0, 1)
+            fetch(b, t, 0)
+            fetch(b, t, 1)
+        for h in range(2):
+            quantise_x(1, h)
+        for h in range(2):
+            scores(h)

@@ -19,6 +19,7 @@ PACK = 4
 PASS = P * PACK
 QUADS = 4
 HALF = PICK // 2
+QUARTER = PICK // 4
 
 FLOPS = 2 * (2 * K * H * S + K2 * H * S + 2 * H * N * PICK)
 
@@ -41,16 +42,13 @@ def tile_list_roast_profile_shelf_kernel(
             nc.sync.dma_start(tile[:], src)
             return tile
 
-        def big(shape, dtype, name):
-            return ring.tile(shape, dtype, name=name, tag="big", bufs=4, align_bytes=64)
-
-        def load_table_words(src, name):
-            tile = big([P, T], I32, name)
+        def load_table_words(src, name, tag):
+            tile = keep.tile([P, T], I32, name=name, tag=tag, align_bytes=64)
             nc.sync.dma_start(tile[:], src.rearrange("p t i -> p (t i)").bitcast(I32))
             return tile
 
-        def zeroed(engine, width, name):
-            tile = keep.tile([P, width], U8, name=name, align_bytes=64)
+        def zeroed(engine, width, name, tag=None):
+            tile = keep.tile([P, width], U8, name=name, tag=tag or name, align_bytes=64)
             engine.memset(tile[:].bitcast(I32), 0)
             return tile
 
@@ -68,20 +66,22 @@ def tile_list_roast_profile_shelf_kernel(
                 queue.dma_start(tile[32 * q : 32 * q + 32, :, :], rows[:, t0:t1, :])
 
         page_rows = page0.rearrange("(b p t) c -> b t p c", p=P, t=PACK)
-        pages = {}
+        pages, page_tag = {}, {}
 
-        def load_page(b, t):
-            pages[b, t] = keep.tile([P, T2], F32, name=f"page{b}{t}")
+        def load_page(b, t, tag=None):
+            page_tag[b, t] = tag or f"page{b}{t}"
+            pages[b, t] = keep.tile([P, T2], F32, name=f"page{b}{t}", tag=page_tag[b, t], align_bytes=64)
             nc.sync.dma_start(pages[b, t][:], page_rows[b, t])
 
-        def load_float_weight(src, name):
-            tile = big([P, PACK, 512], F32, name)
+        def load_float_weight(src, name, tag):
+            tile = keep.tile([P, PACK, 512], F32, name=name, tag=tag, align_bytes=64)
             nc.sync.dma_start(tile[:], src.rearrange("(p i) c -> p i c", i=PACK))
             return tile
 
-        def quantise(src, name):
-            codes = keep.tile([P, 512], U32, name=name + "_codes", align_bytes=64)
-            scales = keep.tile([P, 512], U8, name=name + "_scales", align_bytes=64)
+        def quantise(src, name, tag):
+            width = src.shape[1] // PACK
+            codes = keep.tile([P, width], U32, name=name + "_codes", tag=tag + "_codes", align_bytes=64)
+            scales = keep.tile([P, width], U8, name=name + "_scales", tag=tag + "_scales", align_bytes=64)
             nc.vector.quantize_mx(out=codes[:].bitcast(FP8X4), scales=scales[:], in_=src)
             return codes, scales
 
@@ -92,67 +92,63 @@ def tile_list_roast_profile_shelf_kernel(
                     src[4 * q : 4 * q + 4, :].bitcast(I32).partition_broadcast(8),
                 )
 
-        wa_plane_raw = zeroed(nc.vector, 2 * H, "wa_plane_raw")
+        def load_two_planes(tile, src):
+            for q in range(QUADS):
+                nc.sync.dma_start(tile[32 * q : 32 * q + 8, :].bitcast(I32), src[:, 4 * q : 4 * q + 4, :].bitcast(I32))
+
+        def move_second_plane(dst, src):
+            for q in range(QUADS):
+                nc.sync.dma_start(dst[32 * q : 32 * q + 4, :].bitcast(I32), src[32 * q + 4 : 32 * q + 8, :].bitcast(I32))
+
         t_plane = zeroed(nc.vector, T, "t_plane")
+        wa_plane_raw = zeroed(nc.vector, H, "wa_plane_raw")
         v_plane1 = zeroed(nc.vector, S, "v_plane1")
-        w5_plane = zeroed(nc.vector, 2 * N, "w5_plane")
+        wa_plane1 = zeroed(nc.vector, H, "wa_plane1")
 
         idx2 = load_list(offs2, "idx2")
-        t2_plane = keep.tile([P, T], U8, name="t2_plane", align_bytes=64)
+        t2_plane = keep.tile([P, T], U8, name="t2_plane", tag="t2_plane", align_bytes=64)
         load_plane_filled(t2_plane, tab2_scales[0])
-        t2_words = load_table_words(tab2_words[0], "t2_words")
-        wc_raw = ring.tile([P, H], I32, name="wc_raw", tag="wraw", bufs=1, align_bytes=64)
+        t2_words = load_table_words(tab2_words[0], "t2_words", "t2_words")
+        wc_raw = keep.tile([P, H], I32, name="wc_raw", tag="wc_raw", align_bytes=64)
         nc.sync.dma_start(wc_raw[:], wc_words[0].rearrange("p c i -> p (c i)").bitcast(I32))
-        wc_plane_raw = keep.tile([P, H], U8, name="wc_plane_raw", align_bytes=64)
+        wc_plane_raw = keep.tile([P, H], U8, name="wc_plane_raw", tag="wc_plane_raw", align_bytes=64)
         load_plane_filled(wc_plane_raw, wc_scales[0])
-        load_page(0, 0)
         gc_col = keep.tile([P, 2, PACK], F32, name="gc_col")
         nc.sync.dma_start(gc_col[:], gc.rearrange("(b p t) -> p b t", p=P, t=PACK))
+        load_page(0, 0)
         idx4 = load_list(offs4, "idx4")
-        wg2_first = keep.tile([P, 1, S], F32, name="wg2_first")
+        wg2_first = keep.tile([P, 1, S], F32, name="wg2_first", tag="wg2_first", align_bytes=64)
         load_dealt_gain(nc.sync, wg2_first, wg2, 0, 1)
-        idx = load_list(offs, "idx")
-        load_plane(nc.gpsimd, wa_plane_raw, wa_scales)
-        for q in range(QUADS):
-            nc.gpsimd.dma_start(
-                t_plane[32 * q : 32 * q + 8, :].bitcast(I32), tab_scales[:, 4 * q : 4 * q + 4, :].bitcast(I32)
-            )
         load_page(1, 0)
+        idx = load_list(offs, "idx")
         wg2_rest = keep.tile([P, PACK - 1, S], F32, name="wg2_rest")
         load_dealt_gain(nc.sync, wg2_rest, wg2, 1, PACK)
         load_page(0, 1)
-        t_words = [load_table_words(tab_words[0], "t_words0")]
-        load_page(0, 2)
-        t_words.append(load_table_words(tab_words[1], "t_words1"))
-        load_page(0, 3)
+        v_planes = keep.tile([P, S], U8, name="v_planes", align_bytes=64)
+        wa_planes = keep.tile([P, H], U8, name="wa_planes", align_bytes=64)
+        v_scales = (v_planes, v_plane1)
+        wa_scale = (wa_planes, wa_plane1)
         wb_raw = {}
 
         def load_wb(a, b):
-            wb_raw[a, b] = load_float_weight(wb[PASS * a : PASS * (a + 1), 512 * b : 512 * (b + 1)], f"wb_raw{a}{b}")
+            wb_raw[a, b] = load_float_weight(wb[PASS * a : PASS * (a + 1), 512 * b : 512 * (b + 1)], f"wb_raw{a}{b}", f"wb_raw{a}")
 
-        load_wb(0, 0)
-        wa_raw = ring.tile([P, H], I32, name="wa_raw", tag="wraw", bufs=1, align_bytes=64)
-        nc.sync.dma_start(
-            wa_raw[:].rearrange("p (a c) -> p a c", a=2), wa_words.bitcast(I32).rearrange("a p c -> p a c")
-        )
-        load_wb(1, 0)
-        load_page(1, 1)
-        wg1_first = keep.tile([P, 1, S], F32, name="wg1_first")
-        load_dealt_gain(nc.sync, wg1_first, wg1, 0, 1)
         idx3 = load_list(offs3, "idx3")
-        load_page(1, 2)
         idx5 = load_list(offs5, "idx5")
+        load_page(0, 2)
         gx_col = keep.tile([P, 2, PACK], F32, name="gx_col")
         nc.sync.dma_start(gx_col[:], gx.rearrange("(b p t) -> p b t", p=P, t=PACK))
-        wg1_rest = keep.tile([P, PACK - 1, S], F32, name="wg1_rest")
-        load_dealt_gain(nc.sync, wg1_rest, wg1, 1, PACK)
-        load_page(1, 3)
+        load_two_planes(wa_plane_raw, wa_scales)
+        load_wb(0, 0)
+        load_two_planes(t_plane, tab_scales)
+        load_wb(1, 0)
+        t_words = [load_table_words(tab_words[0], "t_words0", "t_words0")]
 
         v2_plane = keep.tile([P, S], U8, name="v2_plane", align_bytes=64)
         nc.vector.tensor_copy(v2_plane[:], t2_plane[:].indirect(idx2[:]))
-        v2_codes = keep.tile([P, S], U32, name="v2_codes", align_bytes=64)
+        v2_codes = keep.tile([P, S], U32, name="v2_codes", tag="v2_codes", align_bytes=64)
         nc.vector.tensor_copy(v2_codes[:], t2_words[:].bitcast(U32).indirect(idx2[:]))
-        wc_plane = keep.tile([P, H], U8, name="wc_plane", align_bytes=64)
+        wc_plane = keep.tile([P, H], U8, name="wc_plane", tag="wc_plane", align_bytes=64)
         wc_codes = keep.tile([P, H], U32, name="wc_codes", align_bytes=64)
         for b in range(2):
             nc.vector.tensor_copy(
@@ -164,88 +160,107 @@ def tile_list_roast_profile_shelf_kernel(
                 wc_raw[:, 512 * b : 512 * (b + 1)].bitcast(U32).rearrange("p (m t) -> p m t", t=PACK),
             )
 
-        def curve(b, t, u):
+        def curve(b, t, feature=None):
             cols = slice(512 * b + P * t, 512 * b + P * (t + 1))
-            c = bank(u % 2)
+            c = bank(0)
             nc.tensor.matmul_mx(
                 out=c[:], lhsT=wc_codes[:, cols].bitcast(FP8X4), lhsT_scale=wc_plane[:, cols],
                 rhs=v2_codes[:].bitcast(FP8X4), rhs_scale=v2_plane[:], start=True, stop=True,
             )
-            size = ring.tile([P, S], F32, name="size", tag="staged", bufs=2)
-            nc.scalar.activation(size[:], c[:], ACT.Abs)
-            feature = ring.tile([P, S], F32, name="feature", tag="result", bufs=8)
-            nc.scalar.activation(feature[:], size[:], ACT.Exp, scale=-1.0)
-            nc.scalar.activation(feature[:], feature[:], ACT.Copy, scale=gc_col[:, b, t : t + 1])
+            if feature is None:
+                feature = ring.tile([P, S], F32, name="feature", tag="result", bufs=8)
+            halves = (slice(0, S // 2), slice(S // 2, S))
+            for h in halves:
+                nc.scalar.activation(feature[:, h], c[:, h], ACT.Abs)
+            for h in halves:
+                nc.scalar.activation(feature[:, h], feature[:, h], ACT.Exp, scale=-1.0)
+            for h in halves:
+                nc.scalar.activation(feature[:, h], feature[:, h], ACT.Copy, scale=gc_col[:, b, t : t + 1])
             gain = wg2_first[:, 0, :] if t == 0 else wg2_rest[:, t - 1, :]
             nc.vector.tensor_tensor(pages[b, t][:].indirect(idx4[:]), feature[:], gain, ALU.mult)
 
-        def round_wb(raw, name):
-            rounded = ring.tile([P, 512 * PACK], BF16, name=name, tag="rounded", bufs=4, align_bytes=64)
+        def round_wb(raw, name, tag):
+            rounded = keep.tile([P, 512 * PACK], BF16, name=name, tag=tag, align_bytes=64)
             nc.scalar.copy(
                 rounded[:].rearrange("p (t m i) -> p m t i", t=PACK, i=PACK),
                 raw[:].rearrange("p i (m t) -> p m t i", t=PACK),
             )
             return rounded
 
-        def round_w4(raw, name):
-            rounded = ring.tile([P, 512 * PACK], BF16, name=name, tag="rounded", bufs=4, align_bytes=64)
+        def round_w4(raw, name, tag):
+            rounded = keep.tile([P, 512 * PACK], BF16, name=name, tag=tag, align_bytes=64)
             nc.scalar.copy(rounded[:].rearrange("p (c i) -> p c i", i=PACK), raw[:].rearrange("p i c -> p c i"))
             return rounded
 
-        wb_q, w4_q, v_codes = {}, {}, {}
+        wb_q, w4_bf, w4_q, v_codes = {}, {}, {}, {}
 
         def prepare_wb(a, b):
-            wb_q[a, b] = quantise(round_wb(wb_raw[a, b], f"wb_bf{a}{b}")[:], f"wb{a}{b}")
+            wb_q[a, b] = quantise(round_wb(wb_raw[a, b], f"wb_bf{a}{b}", f"bf{a}{b}")[:], f"wb{a}{b}", f"wb{a}{b}")
 
         def prepare_w4(b):
-            raw = load_float_weight(w4[PASS * b : PASS * (b + 1), :], f"w4_raw{b}")
-            w4_q[b] = quantise(round_w4(raw, f"w4_bf{b}")[:], f"w4{b}")
+            raw = load_float_weight(w4[PASS * b : PASS * (b + 1), :], f"w4_raw{b}", f"wb_raw{b}")
+            w4_bf[b] = round_w4(raw, f"w4_bf{b}", f"bf{b}0")
 
         def gather_v(a):
             v_codes[a] = keep.tile([P, S], U32, name=f"v_codes{a}", align_bytes=64)
             nc.vector.tensor_copy(v_codes[a][:], t_words[a][:].bitcast(U32).indirect(idx[:]))
 
-        curve(0, 0, 0)
-        v_planes = keep.tile([P, S], U8, name="v_planes", align_bytes=64)
+        curve(0, 0)
+        curve(1, 0)
         nc.vector.tensor_copy(v_planes[:], t_plane[:].indirect(idx[:]))
-        for q in range(QUADS):
-            nc.gpsimd.dma_start(
-                v_plane1[32 * q : 32 * q + 4, :].bitcast(I32), v_planes[32 * q + 4 : 32 * q + 8, :].bitcast(I32)
-            )
-        wa_plane = keep.tile([P, 2 * H], U8, name="wa_plane", align_bytes=64)
         nc.vector.tensor_copy(
-            wa_plane[:].rearrange("p (g t m) -> p g t m", g=4, t=PACK),
-            wa_plane_raw[:].rearrange("p (g m t) -> p g t m", g=4, t=PACK),
+            wa_planes[:].rearrange("p (b t m) -> p b t m", b=2, t=PACK),
+            wa_plane_raw[:].rearrange("p (b m t) -> p b t m", b=2, t=PACK),
         )
-        curve(1, 0, 1)
-        curve(0, 1, 2)
-        gather_v(0)
-        curve(0, 2, 3)
-        gather_v(1)
-        curve(0, 3, 4)
+        t_words.append(load_table_words(tab_words[1], "t_words1", "t2_plane"))
+        wa_raw = keep.tile([P, H], I32, name="wa_raw", tag="t2_words", align_bytes=64)
+        nc.sync.dma_start(
+            wa_raw[:].rearrange("p (a c) -> p a c", a=2), wa_words.bitcast(I32).rearrange("a p c -> p a c")
+        )
+        load_page(0, 3, "wc_raw")
+        move_second_plane(wa_plane1, wa_planes)
+        load_page(1, 1, "wa_plane_raw")
+        move_second_plane(v_plane1, v_planes)
+        wg1_all = keep.tile([P, PACK, S], F32, name="wg1_all", tag="t_plane", align_bytes=64)
+        load_dealt_gain(nc.sync, wg1_all, wg1, 0, PACK)
+        curve(0, 1)
         prepare_wb(0, 0)
+        curve(0, 2)
+        prepare_wb(1, 0)
         wa_codes = keep.tile([P, 2 * H], U16, name="wa_codes", align_bytes=64)
         nc.scalar.copy(
             wa_codes[:].rearrange("p (g t m) -> p g t m", g=4, t=PACK),
             wa_raw[:].bitcast(U16).rearrange("p (g m t) -> p g t m", g=4, t=PACK),
         )
-        prepare_wb(1, 0)
-        curve(1, 1, 5)
-        curve(1, 2, 6)
-        curve(1, 3, 7)
+        for a in range(2):
+            gather_v(a)
+            load_wb(a, 1)
+        load_page(1, 2, "t_words0")
+        curve(0, 3)
+        curve(1, 1)
+        late = keep.tile([P, 2, S], F32, name="late", tag="t2_words", align_bytes=64)
+        curve(1, 2, late[:, 0, :])
+        load_page(1, 3, "t2_plane")
+        curve(1, 3, late[:, 1, :])
+        order = [(b, t) for b in range(2) for t in range(PACK)]
+        lower = {}
+        for b, t in order:
+            pa = bank(4 + t % 2)
+            for a in (1, 0):
+                cols = slice(H * a + 512 * b + P * t, H * a + 512 * b + P * (t + 1))
+                nc.tensor.matmul_mx(
+                    out=pa[:], lhsT=wa_codes[:, cols].bitcast(FP4X4), lhsT_scale=wa_scale[a][:, 512 * b + P * t : 512 * b + P * (t + 1)],
+                    rhs=v_codes[a][:].bitcast(FP8X4), rhs_scale=v_scales[a][:], start=a == 1, stop=a == 0,
+                )
+            lower[b, t] = ring.tile([P, S], F32, name="lower", tag="result", bufs=8)
+            nc.scalar.copy(lower[b, t][:], pa[:])
+        prepare_wb(0, 1)
+        prepare_wb(1, 1)
 
-        v_scales = (v_planes, v_plane1)
         x_bf, x_q = {}, {}
 
         def bean_features(b, t):
-            u = PACK * b + t
-            pa, pb = bank(2 + u % 2), bank(4 + u % 2)
-            for a in range(2):
-                cols = slice(H * a + 512 * b + P * t, H * a + 512 * b + P * (t + 1))
-                nc.tensor.matmul_mx(
-                    out=pa[:], lhsT=wa_codes[:, cols].bitcast(FP4X4), lhsT_scale=wa_plane[:, cols],
-                    rhs=v_codes[a][:].bitcast(FP8X4), rhs_scale=v_scales[a][:], start=a == 0, stop=a == 1,
-                )
+            pb = bank(6 + t % 2)
             cols = slice(P * t, P * (t + 1))
             for a in range(2):
                 codes, scales = wb_q[a, b]
@@ -253,74 +268,88 @@ def tile_list_roast_profile_shelf_kernel(
                     out=pb[:], lhsT=codes[:, cols].bitcast(FP8X4), lhsT_scale=scales[:, cols],
                     rhs=v_codes[a][:].bitcast(FP8X4), rhs_scale=v_scales[a][:], start=a == 0, stop=a == 1,
                 )
-            first = ring.tile([P, S], F32, name="first", tag="staged", bufs=2)
-            nc.scalar.copy(first[:], pa[:])
-            lower = ring.tile([P, S], F32, name="lower", tag="result", bufs=8)
-            nc.vector.tensor_tensor(lower[:], pb[:], first[:], ALU.min)
-            return lower
+            u = PACK * b + t
+            first = lower[b, t]
+            if u >= 2:
+                done = order[u - 1 if u + 1 == len(order) else u - 2]
+                lower[b, t] = keep.tile([P, S], F32, name="h1", tag=page_tag[done], align_bytes=64)
+            nc.vector.tensor_tensor(lower[b, t][:], pb[:], first[:], ALU.min)
 
-        def put_bean(b, t, lower):
-            gain = wg1_first[:, 0, :] if t == 0 else wg1_rest[:, t - 1, :]
-            nc.vector.tensor_tensor(pages[b, t][:].indirect(idx3[:]), lower[:], gain, ALU.mult)
+        def put_bean(b, t):
+            gain = wg1_all[:, t, :]
+            nc.vector.tensor_tensor(pages[b, t][:].indirect(idx3[:]), lower[b, t][:], gain, ALU.mult)
 
-        def fetch(b, t, h):
-            if t == 0:
-                x_bf[b, h] = ring.tile([P, HALF, PACK], BF16, name=f"x_bf{b}{h}", tag="x_bf", bufs=4, align_bytes=64)
-            picked = ring.tile([P, HALF], F32, name="picked", tag="picked", bufs=4)
-            w = HALF // 16
-            nc.vector.tensor_copy(picked[:], pages[b, t][:].indirect(idx5[:, w * h : w * (h + 1)]))
-            nc.scalar.activation(x_bf[b, h][:, :, t], picked[:], ACT.Copy, scale=gx_col[:, b, t : t + 1])
+        x_width = (HALF, QUARTER)
+
+        def fetch(b, t, j0, j1):
+            w = x_width[b]
+            picked = ring.tile([P, j1 - j0], F32, name="picked", tag="picked", bufs=4)
+            nc.vector.tensor_copy(picked[:], pages[b, t][:].indirect(idx5[:, j0 // 16 : j1 // 16]))
+            for j in range(j0, j1, w):
+                if t == 0:
+                    tag = f"wb_raw{j // w}" if b == 0 else f"x_bf{j // w}"
+                    x_bf[b, j // w] = keep.tile([P, w, PACK], BF16, name=f"x_bf{b}{j // w}", tag=tag, align_bytes=64)
+                nc.scalar.activation(
+                    x_bf[b, j // w][:, :, t], picked[:, j - j0 : j - j0 + w], ACT.Copy, scale=gx_col[:, b, t : t + 1]
+                )
 
         def quantise_x(b, h):
-            x_q[b, h] = quantise(x_bf[b, h][:].rearrange("p c i -> p (c i)"), f"x{b}{h}")
+            x_q[b, h] = quantise(x_bf[b, h][:].rearrange("p c i -> p (c i)"), f"x{b}{h}", f"x{b}{h}")
 
-        w5_codes = keep.tile([P, 2 * N], U16, name="w5_codes", align_bytes=64)
+        w5_codes = keep.tile([P, 2 * N], U16, name="w5_codes", tag="v2_codes", align_bytes=64)
 
-        def scores(h):
-            for n in range(N // P):
-                y1, y2 = bank(2 * n), bank(2 * n + 1)
-                cols = slice(P * n, P * (n + 1))
+        def scores(q):
+            for g in range(2):
+                y1, y2 = bank(4 * (q % 2) + 2 * g), bank(4 * (q % 2) + 2 * g + 1)
                 for b in range(2):
-                    wide = slice(N * b + P * n, N * b + P * (n + 1))
+                    h, j = divmod(QUARTER * q, x_width[b])
                     codes, scales = x_q[b, h]
-                    nc.tensor.matmul_mx(
-                        out=y2[:], lhsT=w5_codes[:, wide].bitcast(FP4X4), lhsT_scale=w5_plane[:, wide],
-                        rhs=codes[:].bitcast(FP8X4), rhs_scale=scales[:], start=b == 0, stop=b == 1,
-                    )
-                    nc.tensor.matmul_mx(
-                        out=y1[:], lhsT=w4_q[b][0][:, cols].bitcast(FP8X4), lhsT_scale=w4_q[b][1][:, cols],
-                        rhs=codes[:].bitcast(FP8X4), rhs_scale=scales[:], start=b == 0, stop=b == 1,
-                    )
-                second = ring.tile([P, HALF], F32, name="second", tag="staged", bufs=2)
+                    moving = dict(rhs=codes[:, j : j + QUARTER].bitcast(FP8X4), rhs_scale=scales[:, j : j + QUARTER])
+                    for i in range(2):
+                        n = 2 * g + i
+                        wide = slice(N * b + P * n, N * b + P * (n + 1))
+                        nc.tensor.matmul_mx(
+                            out=y2[:, QUARTER * i : QUARTER * (i + 1)],
+                            lhsT=w5_codes[:, wide].bitcast(FP4X4), lhsT_scale=w5_plane[:, wide],
+                            start=b + i == 0, stop=b + i == 2, **moving,
+                        )
+                    for i in range(2):
+                        cols = slice(P * (2 * g + i), P * (2 * g + i + 1))
+                        nc.tensor.matmul_mx(
+                            out=y1[:, QUARTER * i : QUARTER * (i + 1)],
+                            lhsT=w4_q[b][0][:, cols].bitcast(FP8X4), lhsT_scale=w4_q[b][1][:, cols],
+                            start=b + i == 0, stop=b + i == 2, **moving,
+                        )
+                second = ring.tile([P, HALF], F32, name="second", tag="staged", bufs=4)
                 nc.scalar.copy(second[:], y2[:])
                 larger = ring.tile([P, HALF], F32, name="larger", tag="result", bufs=8)
                 nc.vector.tensor_tensor(larger[:], y1[:], second[:], ALU.max)
-                nc.sync.dma_start(out[cols, HALF * h : HALF * (h + 1)], larger[:])
-
-        order = [(b, t) for b in range(2) for t in range(PACK)]
-        lower = bean_features(0, 0)
-        for u, (b, t) in enumerate(order):
-            put_bean(b, t, lower)
-            if u == 0:
-                for a in range(2):
-                    load_wb(a, 1)
-                    prepare_wb(a, 1)
-            if u == 1:
-                prepare_w4(0)
-                prepare_w4(1)
                 nc.sync.dma_start(
-                    w5_codes[:].bitcast(I32).rearrange("p (a c) -> p a c", a=2),
-                    w5_words.bitcast(I32).rearrange("a p c -> p a c"),
+                    out[2 * P * g : 2 * P * (g + 1), QUARTER * q : QUARTER * (q + 1)].rearrange("(i p) c -> p i c", p=P),
+                    larger[:].rearrange("p (i c) -> p i c", i=2),
                 )
-                load_plane(nc.sync, w5_plane, w5_scales)
+
+        w5_plane = zeroed(nc.vector, 2 * N, "w5_plane", "wc_plane_raw")
+        load_plane(nc.sync, w5_plane, w5_scales)
+        prepare_w4(0)
+        prepare_w4(1)
+        nc.sync.dma_start(
+            w5_codes[:].bitcast(I32).rearrange("p (a c) -> p a c", a=2),
+            w5_words.bitcast(I32).rearrange("a p c -> p a c"),
+        )
+        bean_features(0, 0)
+        for u, (b, t) in enumerate(order):
+            put_bean(b, t)
+            if u + 2 < len(order):
+                bean_features(*order[u + 1])
             if u + 1 < len(order):
-                lower = bean_features(*order[u + 1])
-            if u == PACK:
-                quantise_x(0, 0)
-                quantise_x(0, 1)
-            fetch(b, t, 0)
-            fetch(b, t, 1)
-        for h in range(2):
-            quantise_x(1, h)
-        for h in range(2):
-            scores(h)
+                fetch(b, t, 0, PICK)
+            if u + 2 == len(order):
+                bean_features(*order[u + 1])
+                for a in range(2):
+                    w4_q[a] = quantise(w4_bf[a][:], f"w4{a}", f"wb{a}1")
+                    quantise_x(0, a)
+        for q in range(PICK // QUARTER):
+            fetch(1, PACK - 1, QUARTER * q, QUARTER * (q + 1))
+            quantise_x(1, q)
+            scores(q)

@@ -66,6 +66,7 @@ def tile_list_roast_profile_shelf_kernel(
                 queue.dma_start(tile[32 * q : 32 * q + 32, :, :], rows[:, t0:t1, :])
 
         page_rows = page0.rearrange("(b p t) c -> b t p c", p=P, t=PACK)
+        table_tag = ("wa_plane_raw", "wb_raw1")
         pages, page_tag = {}, {}
 
         def load_page(b, t, tag=None):
@@ -120,10 +121,13 @@ def tile_list_roast_profile_shelf_kernel(
         wg2_first = keep.tile([P, 1, S], F32, name="wg2_first", tag="wg2_first", align_bytes=64)
         load_dealt_gain(nc.sync, wg2_first, wg2, 0, 1)
         load_page(1, 0)
-        idx = load_list(offs, "idx")
-        wg2_rest = keep.tile([P, PACK - 1, S], F32, name="wg2_rest")
-        load_dealt_gain(nc.sync, wg2_rest, wg2, 1, PACK)
+        wg2_second = keep.tile([P, 1, S], F32, name="wg2_second")
+        load_dealt_gain(nc.sync, wg2_second, wg2, 1, 2)
         load_page(0, 1)
+        idx = load_list(offs, "idx")
+        load_page(1, 1)
+        wg2_rest = keep.tile([P, 2, S], F32, name="wg2_rest", tag="wg2_rest", align_bytes=64)
+        load_dealt_gain(nc.sync, wg2_rest, wg2, 2, PACK)
         v_planes = keep.tile([P, S], U8, name="v_planes", align_bytes=64)
         wa_planes = keep.tile([P, H], U8, name="wa_planes", align_bytes=64)
         v_scales = (v_planes, v_plane1)
@@ -131,18 +135,20 @@ def tile_list_roast_profile_shelf_kernel(
         wb_raw = {}
 
         def load_wb(a, b):
-            wb_raw[a, b] = load_float_weight(wb[PASS * a : PASS * (a + 1), 512 * b : 512 * (b + 1)], f"wb_raw{a}{b}", f"wb_raw{a}")
+            wb_raw[a, b] = load_float_weight(wb[PASS * a : PASS * (a + 1), 512 * b : 512 * (b + 1)], f"wb_raw{a}{b}", (f"wb_raw{a}", ("wb_raw1", "t_words0")[a])[b])
 
-        idx3 = load_list(offs3, "idx3")
-        idx5 = load_list(offs5, "idx5")
         load_page(0, 2)
-        gx_col = keep.tile([P, 2, PACK], F32, name="gx_col")
-        nc.sync.dma_start(gx_col[:], gx.rearrange("(b p t) -> p b t", p=P, t=PACK))
         load_two_planes(wa_plane_raw, wa_scales)
         load_wb(0, 0)
         load_two_planes(t_plane, tab_scales)
+        load_page(1, 2)
+        idx3 = load_list(offs3, "idx3")
+        idx5 = load_list(offs5, "idx5")
         load_wb(1, 0)
+        gx_col = keep.tile([P, 2, PACK], F32, name="gx_col")
+        nc.sync.dma_start(gx_col[:], gx.rearrange("(b p t) -> p b t", p=P, t=PACK))
         t_words = [load_table_words(tab_words[0], "t_words0", "t_words0")]
+        load_page(0, 3, "t2_words")
 
         v2_plane = keep.tile([P, S], U8, name="v2_plane", align_bytes=64)
         nc.vector.tensor_copy(v2_plane[:], t2_plane[:].indirect(idx2[:]))
@@ -160,15 +166,14 @@ def tile_list_roast_profile_shelf_kernel(
                 wc_raw[:, 512 * b : 512 * (b + 1)].bitcast(U32).rearrange("p (m t) -> p m t", t=PACK),
             )
 
-        def curve(b, t, feature=None):
+        def curve(b, t):
             cols = slice(512 * b + P * t, 512 * b + P * (t + 1))
             c = bank(0)
             nc.tensor.matmul_mx(
                 out=c[:], lhsT=wc_codes[:, cols].bitcast(FP8X4), lhsT_scale=wc_plane[:, cols],
                 rhs=v2_codes[:].bitcast(FP8X4), rhs_scale=v2_plane[:], start=True, stop=True,
             )
-            if feature is None:
-                feature = ring.tile([P, S], F32, name="feature", tag="result", bufs=8)
+            feature = ring.tile([P, S], F32, name="feature", tag="result", bufs=8)
             halves = (slice(0, S // 2), slice(S // 2, S))
             for h in halves:
                 nc.scalar.activation(feature[:, h], c[:, h], ACT.Abs)
@@ -176,7 +181,7 @@ def tile_list_roast_profile_shelf_kernel(
                 nc.scalar.activation(feature[:, h], feature[:, h], ACT.Exp, scale=-1.0)
             for h in halves:
                 nc.scalar.activation(feature[:, h], feature[:, h], ACT.Copy, scale=gc_col[:, b, t : t + 1])
-            gain = wg2_first[:, 0, :] if t == 0 else wg2_rest[:, t - 1, :]
+            gain = (wg2_first[:, 0, :], wg2_second[:, 0, :], wg2_rest[:, 0, :], wg2_rest[:, 1, :])[t]
             nc.vector.tensor_tensor(pages[b, t][:].indirect(idx4[:]), feature[:], gain, ALU.mult)
 
         def round_wb(raw, name, tag):
@@ -198,8 +203,8 @@ def tile_list_roast_profile_shelf_kernel(
             wb_q[a, b] = quantise(round_wb(wb_raw[a, b], f"wb_bf{a}{b}", f"bf{a}{b}")[:], f"wb{a}{b}", f"wb{a}{b}")
 
         def prepare_w4(b):
-            raw = load_float_weight(w4[PASS * b : PASS * (b + 1), :], f"w4_raw{b}", f"wb_raw{b}")
-            w4_bf[b] = round_w4(raw, f"w4_bf{b}", f"bf{b}0")
+            raw = load_float_weight(w4[PASS * b : PASS * (b + 1), :], f"w4_raw{b}", table_tag[b])
+            w4_bf[b] = round_w4(raw, f"w4_bf{b}", ("wg2_first", "wc_raw")[b])
 
         def gather_v(a):
             v_codes[a] = keep.tile([P, S], U32, name=f"v_codes{a}", align_bytes=64)
@@ -207,41 +212,39 @@ def tile_list_roast_profile_shelf_kernel(
 
         curve(0, 0)
         curve(1, 0)
+        curve(0, 1)
+        curve(1, 1)
+        curve(0, 2)
         nc.vector.tensor_copy(v_planes[:], t_plane[:].indirect(idx[:]))
         nc.vector.tensor_copy(
             wa_planes[:].rearrange("p (b t m) -> p b t m", b=2, t=PACK),
             wa_plane_raw[:].rearrange("p (b m t) -> p b t m", b=2, t=PACK),
         )
-        t_words.append(load_table_words(tab_words[1], "t_words1", "t2_plane"))
-        wa_raw = keep.tile([P, H], I32, name="wa_raw", tag="t2_words", align_bytes=64)
+        t_words.append(load_table_words(tab_words[1], "t_words1", "wa_plane_raw"))
+        wa_raw = keep.tile([P, H], I32, name="wa_raw", tag="t_plane", align_bytes=64)
         nc.sync.dma_start(
             wa_raw[:].rearrange("p (a c) -> p a c", a=2), wa_words.bitcast(I32).rearrange("a p c -> p a c")
         )
-        load_page(0, 3, "wc_raw")
         move_second_plane(wa_plane1, wa_planes)
-        load_page(1, 1, "wa_plane_raw")
         move_second_plane(v_plane1, v_planes)
-        wg1_all = keep.tile([P, PACK, S], F32, name="wg1_all", tag="t_plane", align_bytes=64)
-        load_dealt_gain(nc.sync, wg1_all, wg1, 0, PACK)
-        curve(0, 1)
         prepare_wb(0, 0)
-        curve(0, 2)
+        load_page(1, 3, "wb_raw0")
+        wg1_first = keep.tile([P, 2, S], F32, name="wg1_first", tag="bf00", align_bytes=64)
+        load_dealt_gain(nc.sync, wg1_first, wg1, 0, 2)
+        curve(1, 2)
         prepare_wb(1, 0)
         wa_codes = keep.tile([P, 2 * H], U16, name="wa_codes", align_bytes=64)
         nc.scalar.copy(
             wa_codes[:].rearrange("p (g t m) -> p g t m", g=4, t=PACK),
             wa_raw[:].bitcast(U16).rearrange("p (g m t) -> p g t m", g=4, t=PACK),
         )
+        wg1_rest = keep.tile([P, 2, S], F32, name="wg1_rest", tag="bf10", align_bytes=64)
+        load_dealt_gain(nc.sync, wg1_rest, wg1, 2, PACK)
         for a in range(2):
             gather_v(a)
             load_wb(a, 1)
-        load_page(1, 2, "t_words0")
         curve(0, 3)
-        curve(1, 1)
-        late = keep.tile([P, 2, S], F32, name="late", tag="t2_words", align_bytes=64)
-        curve(1, 2, late[:, 0, :])
-        load_page(1, 3, "t2_plane")
-        curve(1, 3, late[:, 1, :])
+        curve(1, 3)
         order = [(b, t) for b in range(2) for t in range(PACK)]
         lower = {}
         for b, t in order:
@@ -254,10 +257,10 @@ def tile_list_roast_profile_shelf_kernel(
                 )
             lower[b, t] = ring.tile([P, S], F32, name="lower", tag="result", bufs=8)
             nc.scalar.copy(lower[b, t][:], pa[:])
-        prepare_wb(0, 1)
-        prepare_wb(1, 1)
+        for a in range(2):
+            prepare_wb(a, 1)
 
-        x_bf, x_q = {}, {}
+        x_rows, x_bf, x_q = {}, {}, {}
 
         def bean_features(b, t):
             pb = bank(6 + t % 2)
@@ -276,27 +279,38 @@ def tile_list_roast_profile_shelf_kernel(
             nc.vector.tensor_tensor(lower[b, t][:], pb[:], first[:], ALU.min)
 
         def put_bean(b, t):
-            gain = wg1_all[:, t, :]
+            gain = (wg1_first, wg1_rest)[t // 2][:, t % 2, :]
             nc.vector.tensor_tensor(pages[b, t][:].indirect(idx3[:]), lower[b, t][:], gain, ALU.mult)
 
         x_width = (HALF, QUARTER)
 
-        def fetch(b, t, j0, j1):
-            w = x_width[b]
-            picked = ring.tile([P, j1 - j0], F32, name="picked", tag="picked", bufs=4)
+        def pick(b, t, j0, j1):
+            picked = ring.tile([P, j1 - j0], F32, name="picked", tag="picked", bufs=3)
             nc.vector.tensor_copy(picked[:], pages[b, t][:].indirect(idx5[:, j0 // 16 : j1 // 16]))
-            for j in range(j0, j1, w):
+            return picked
+
+        def fetch(b, t):
+            w = x_width[b]
+            picked = pick(b, t, 0, PICK)
+            for h in range(PICK // w):
                 if t == 0:
-                    tag = f"wb_raw{j // w}" if b == 0 else f"x_bf{j // w}"
-                    x_bf[b, j // w] = keep.tile([P, w, PACK], BF16, name=f"x_bf{b}{j // w}", tag=tag, align_bytes=64)
+                    tag = table_tag[h] if b == 0 else f"x_rows{h}"
+                    x_rows[b, h] = keep.tile([P, PACK - b, w], BF16, name=f"x_rows{b}{h}", tag=tag, align_bytes=64)
                 nc.scalar.activation(
-                    x_bf[b, j // w][:, :, t], picked[:, j - j0 : j - j0 + w], ACT.Copy, scale=gx_col[:, b, t : t + 1]
+                    x_rows[b, h][:, t, :], picked[:, w * h : w * (h + 1)], ACT.Copy, scale=gx_col[:, b, t : t + 1]
                 )
 
-        def quantise_x(b, h):
-            x_q[b, h] = quantise(x_bf[b, h][:].rearrange("p c i -> p (c i)"), f"x{b}{h}", f"x{b}{h}")
+        def weave(b, h):
+            x_bf[b, h] = keep.tile([P, x_width[b], PACK], BF16, name=f"x_bf{b}{h}", align_bytes=64)
+            nc.scalar.copy(
+                x_bf[b, h][:, :, 0 : PACK - b].rearrange("p (c e) t -> p c t e", e=PACK),
+                x_rows[b, h][:].rearrange("p t (c e) -> p c t e", e=PACK),
+            )
 
-        w5_codes = keep.tile([P, 2 * N], U16, name="w5_codes", tag="v2_codes", align_bytes=64)
+        def quantise_x(b, h):
+            x_q[b, h] = quantise(x_bf[b, h][:].rearrange("p c t -> p (c t)"), f"x{b}{h}", f"x{b}{h}")
+
+        w5_codes = keep.tile([P, 2 * N], U16, name="w5_codes", tag="wg2_rest", align_bytes=64)
 
         def scores(q):
             for g in range(2):
@@ -329,7 +343,7 @@ def tile_list_roast_profile_shelf_kernel(
                     larger[:].rearrange("p (i c) -> p i c", i=2),
                 )
 
-        w5_plane = zeroed(nc.vector, 2 * N, "w5_plane", "wc_plane_raw")
+        w5_plane = zeroed(nc.vector, 2 * N, "w5_plane", "bf01")
         load_plane(nc.sync, w5_plane, w5_scales)
         prepare_w4(0)
         prepare_w4(1)
@@ -343,13 +357,19 @@ def tile_list_roast_profile_shelf_kernel(
             if u + 2 < len(order):
                 bean_features(*order[u + 1])
             if u + 1 < len(order):
-                fetch(b, t, 0, PICK)
+                fetch(b, t)
+            if u + 1 == PACK:
+                for h in range(2):
+                    weave(0, h)
+                    quantise_x(0, h)
             if u + 2 == len(order):
                 bean_features(*order[u + 1])
                 for a in range(2):
                     w4_q[a] = quantise(w4_bf[a][:], f"w4{a}", f"wb{a}1")
-                    quantise_x(0, a)
+                for q in range(PICK // QUARTER):
+                    weave(1, q)
         for q in range(PICK // QUARTER):
-            fetch(1, PACK - 1, QUARTER * q, QUARTER * (q + 1))
+            picked = pick(1, PACK - 1, QUARTER * q, QUARTER * (q + 1))
+            nc.scalar.activation(x_bf[1, q][:, :, PACK - 1], picked[:], ACT.Copy, scale=gx_col[:, 1, PACK - 1 : PACK])
             quantise_x(1, q)
             scores(q)

@@ -79,9 +79,9 @@ def tile_list_roast_profile_shelf_kernel(
             nc.sync.dma_start(tile[:], src.rearrange("(p i) c -> p i c", i=PACK))
             return tile
 
-        def quantise(src, name, tag):
+        def quantise(src, name, tag, codes_tag=None):
             width = src.shape[1] // PACK
-            codes = keep.tile([P, width], U32, name=name + "_codes", tag=tag + "_codes", align_bytes=64)
+            codes = keep.tile([P, width], U32, name=name + "_codes", tag=codes_tag or tag + "_codes", align_bytes=64)
             scales = keep.tile([P, width], U8, name=name + "_scales", tag=tag + "_scales", align_bytes=64)
             nc.vector.quantize_mx(out=codes[:].bitcast(FP8X4), scales=scales[:], in_=src)
             return codes, scales
@@ -135,7 +135,7 @@ def tile_list_roast_profile_shelf_kernel(
         wb_raw = {}
 
         def load_wb(a, b):
-            wb_raw[a, b] = load_float_weight(wb[PASS * a : PASS * (a + 1), 512 * b : 512 * (b + 1)], f"wb_raw{a}{b}", (f"wb_raw{a}", ("wb_raw1", "t_words0")[a])[b])
+            wb_raw[a, b] = load_float_weight(wb[PASS * a : PASS * (a + 1), 512 * b : 512 * (b + 1)], f"wb_raw{a}{b}", (f"wb_raw{a}", ("wb_raw1", "bf10")[a])[b])
 
         load_page(0, 2)
         load_two_planes(wa_plane_raw, wa_scales)
@@ -148,6 +148,10 @@ def tile_list_roast_profile_shelf_kernel(
         gx_col = keep.tile([P, 2, PACK], F32, name="gx_col")
         nc.sync.dma_start(gx_col[:], gx.rearrange("(b p t) -> p b t", p=P, t=PACK))
         t_words = [load_table_words(tab_words[0], "t_words0", "t_words0")]
+        wa_raw = keep.tile([P, H], I32, name="wa_raw", align_bytes=64)
+        nc.sync.dma_start(
+            wa_raw[:].rearrange("p (a c) -> p a c", a=2), wa_words.bitcast(I32).rearrange("a p c -> p a c")
+        )
         load_page(0, 3, "t2_words")
 
         v2_plane = keep.tile([P, S], U8, name="v2_plane", align_bytes=64)
@@ -157,10 +161,11 @@ def tile_list_roast_profile_shelf_kernel(
         wc_plane = keep.tile([P, H], U8, name="wc_plane", tag="wc_plane", align_bytes=64)
         wc_codes = keep.tile([P, H], U32, name="wc_codes", align_bytes=64)
         for b in range(2):
-            nc.vector.tensor_copy(
-                wc_plane[:, 512 * b : 512 * (b + 1)].rearrange("p (t m) -> p t m", t=PACK),
-                wc_plane_raw[:, 512 * b : 512 * (b + 1)].rearrange("p (m t) -> p t m", t=PACK),
-            )
+            for t0, t1 in ((0, 1), (1, PACK)):
+                nc.vector.tensor_copy(
+                    wc_plane[:, 512 * b : 512 * (b + 1)].rearrange("p (t m) -> p t m", t=PACK)[:, t0:t1, :],
+                    wc_plane_raw[:, 512 * b : 512 * (b + 1)].rearrange("p (m t) -> p t m", t=PACK)[:, t0:t1, :],
+                )
             nc.scalar.copy(
                 wc_codes[:, 512 * b : 512 * (b + 1)].rearrange("p (t m) -> p m t", t=PACK),
                 wc_raw[:, 512 * b : 512 * (b + 1)].bitcast(U32).rearrange("p (m t) -> p m t", t=PACK),
@@ -204,7 +209,7 @@ def tile_list_roast_profile_shelf_kernel(
 
         def prepare_w4(b):
             raw = load_float_weight(w4[PASS * b : PASS * (b + 1), :], f"w4_raw{b}", table_tag[b])
-            w4_bf[b] = round_w4(raw, f"w4_bf{b}", ("wg2_first", "wc_raw")[b])
+            w4_bf[b] = round_w4(raw, f"w4_bf{b}", ("bf00", "wc_raw")[b])
 
         def gather_v(a):
             v_codes[a] = keep.tile([P, S], U32, name=f"v_codes{a}", align_bytes=64)
@@ -221,15 +226,11 @@ def tile_list_roast_profile_shelf_kernel(
             wa_plane_raw[:].rearrange("p (b m t) -> p b t m", b=2, t=PACK),
         )
         t_words.append(load_table_words(tab_words[1], "t_words1", "wa_plane_raw"))
-        wa_raw = keep.tile([P, H], I32, name="wa_raw", tag="t_plane", align_bytes=64)
-        nc.sync.dma_start(
-            wa_raw[:].rearrange("p (a c) -> p a c", a=2), wa_words.bitcast(I32).rearrange("a p c -> p a c")
-        )
+        load_page(1, 3, "t_plane")
         move_second_plane(wa_plane1, wa_planes)
         move_second_plane(v_plane1, v_planes)
         prepare_wb(0, 0)
-        load_page(1, 3, "wb_raw0")
-        wg1_first = keep.tile([P, 2, S], F32, name="wg1_first", tag="bf00", align_bytes=64)
+        wg1_first = keep.tile([P, 2, S], F32, name="wg1_first", tag="wb_raw0", align_bytes=64)
         load_dealt_gain(nc.sync, wg1_first, wg1, 0, 2)
         curve(1, 2)
         prepare_wb(1, 0)
@@ -238,11 +239,11 @@ def tile_list_roast_profile_shelf_kernel(
             wa_codes[:].rearrange("p (g t m) -> p g t m", g=4, t=PACK),
             wa_raw[:].bitcast(U16).rearrange("p (g m t) -> p g t m", g=4, t=PACK),
         )
-        wg1_rest = keep.tile([P, 2, S], F32, name="wg1_rest", tag="bf10", align_bytes=64)
-        load_dealt_gain(nc.sync, wg1_rest, wg1, 2, PACK)
         for a in range(2):
             gather_v(a)
             load_wb(a, 1)
+        wg1_rest = keep.tile([P, 2, S], F32, name="wg1_rest", tag="t_words0", align_bytes=64)
+        load_dealt_gain(nc.sync, wg1_rest, wg1, 2, PACK)
         curve(0, 3)
         curve(1, 3)
         order = [(b, t) for b in range(2) for t in range(PACK)]
@@ -255,7 +256,10 @@ def tile_list_roast_profile_shelf_kernel(
                     out=pa[:], lhsT=wa_codes[:, cols].bitcast(FP4X4), lhsT_scale=wa_scale[a][:, 512 * b + P * t : 512 * b + P * (t + 1)],
                     rhs=v_codes[a][:].bitcast(FP8X4), rhs_scale=v_scales[a][:], start=a == 1, stop=a == 0,
                 )
-            lower[b, t] = ring.tile([P, S], F32, name="lower", tag="result", bufs=8)
+            if (b, t) == order[-1]:
+                lower[b, t] = keep.tile([P, S], F32, name="lower", tag="x00_codes", align_bytes=64)
+            else:
+                lower[b, t] = ring.tile([P, S], F32, name="lower", tag="result", bufs=8)
             nc.scalar.copy(lower[b, t][:], pa[:])
         for a in range(2):
             prepare_wb(a, 1)
@@ -285,7 +289,10 @@ def tile_list_roast_profile_shelf_kernel(
         x_width = (HALF, QUARTER)
 
         def pick(b, t, j0, j1):
-            picked = ring.tile([P, j1 - j0], F32, name="picked", tag="picked", bufs=3)
+            if j0 == PICK - QUARTER:
+                picked = keep.tile([P, j1 - j0], F32, name="picked", tag="x_bf11", align_bytes=64)
+            else:
+                picked = ring.tile([P, j1 - j0], F32, name="picked", tag="picked", bufs=3)
             nc.vector.tensor_copy(picked[:], pages[b, t][:].indirect(idx5[:, j0 // 16 : j1 // 16]))
             return picked
 
@@ -301,39 +308,39 @@ def tile_list_roast_profile_shelf_kernel(
                 )
 
         def weave(b, h):
-            x_bf[b, h] = keep.tile([P, x_width[b], PACK], BF16, name=f"x_bf{b}{h}", align_bytes=64)
+            x_bf[b, h] = keep.tile([P, x_width[b], PACK], BF16, name=f"x_bf{b}{h}", tag=f"x_bf{b}{h}", align_bytes=64)
             nc.scalar.copy(
                 x_bf[b, h][:, :, 0 : PACK - b].rearrange("p (c e) t -> p c t e", e=PACK),
                 x_rows[b, h][:].rearrange("p t (c e) -> p c t e", e=PACK),
             )
 
-        def quantise_x(b, h):
-            x_q[b, h] = quantise(x_bf[b, h][:].rearrange("p c t -> p (c t)"), f"x{b}{h}", f"x{b}{h}")
+        def quantise_x(b, h, codes_tag=None):
+            x_q[b, h] = quantise(x_bf[b, h][:].rearrange("p c t -> p (c t)"), f"x{b}{h}", f"x{b}{h}", codes_tag)
 
         w5_codes = keep.tile([P, 2 * N], U16, name="w5_codes", tag="wg2_rest", align_bytes=64)
+
+        def w4_part(b, n):
+            codes, scales = w4_q[b]
+            return codes[:, P * n : P * (n + 1)].bitcast(FP8X4), scales[:, P * n : P * (n + 1)]
+
+        def w5_part(b, n):
+            cols = slice(N * b + P * n, N * b + P * (n + 1))
+            return w5_codes[:, cols].bitcast(FP4X4), w5_plane[:, cols]
 
         def scores(q):
             for g in range(2):
                 y1, y2 = bank(4 * (q % 2) + 2 * g), bank(4 * (q % 2) + 2 * g + 1)
-                for b in range(2):
-                    h, j = divmod(QUARTER * q, x_width[b])
-                    codes, scales = x_q[b, h]
-                    moving = dict(rhs=codes[:, j : j + QUARTER].bitcast(FP8X4), rhs_scale=scales[:, j : j + QUARTER])
-                    for i in range(2):
-                        n = 2 * g + i
-                        wide = slice(N * b + P * n, N * b + P * (n + 1))
-                        nc.tensor.matmul_mx(
-                            out=y2[:, QUARTER * i : QUARTER * (i + 1)],
-                            lhsT=w5_codes[:, wide].bitcast(FP4X4), lhsT_scale=w5_plane[:, wide],
-                            start=b + i == 0, stop=b + i == 2, **moving,
-                        )
-                    for i in range(2):
-                        cols = slice(P * (2 * g + i), P * (2 * g + i + 1))
-                        nc.tensor.matmul_mx(
-                            out=y1[:, QUARTER * i : QUARTER * (i + 1)],
-                            lhsT=w4_q[b][0][:, cols].bitcast(FP8X4), lhsT_scale=w4_q[b][1][:, cols],
-                            start=b + i == 0, stop=b + i == 2, **moving,
-                        )
+                for y, weight in ((y2, w5_part), (y1, w4_part)):
+                    for b in range(2):
+                        h, j = divmod(QUARTER * q, x_width[b])
+                        codes, scales = x_q[b, h]
+                        for i in range(2):
+                            lhsT, lhsT_scale = weight(b, 2 * g + i)
+                            nc.tensor.matmul_mx(
+                                out=y[:, QUARTER * i : QUARTER * (i + 1)], lhsT=lhsT, lhsT_scale=lhsT_scale,
+                                rhs=codes[:, j : j + QUARTER].bitcast(FP8X4), rhs_scale=scales[:, j : j + QUARTER],
+                                start=b + i == 0, stop=b + i == 2,
+                            )
                 second = ring.tile([P, HALF], F32, name="second", tag="staged", bufs=4)
                 nc.scalar.copy(second[:], y2[:])
                 larger = ring.tile([P, HALF], F32, name="larger", tag="result", bufs=8)
@@ -343,7 +350,7 @@ def tile_list_roast_profile_shelf_kernel(
                     larger[:].rearrange("p (i c) -> p i c", i=2),
                 )
 
-        w5_plane = zeroed(nc.vector, 2 * N, "w5_plane", "bf01")
+        w5_plane = zeroed(nc.vector, 2 * N, "w5_plane", "bf11")
         load_plane(nc.sync, w5_plane, w5_scales)
         prepare_w4(0)
         prepare_w4(1)
@@ -361,15 +368,17 @@ def tile_list_roast_profile_shelf_kernel(
             if u + 1 == PACK:
                 for h in range(2):
                     weave(0, h)
-                    quantise_x(0, h)
             if u + 2 == len(order):
                 bean_features(*order[u + 1])
                 for a in range(2):
                     w4_q[a] = quantise(w4_bf[a][:], f"w4{a}", f"wb{a}1")
+                quantise_x(0, 0)
                 for q in range(PICK // QUARTER):
                     weave(1, q)
         for q in range(PICK // QUARTER):
             picked = pick(1, PACK - 1, QUARTER * q, QUARTER * (q + 1))
             nc.scalar.activation(x_bf[1, q][:, :, PACK - 1], picked[:], ACT.Copy, scale=gx_col[:, 1, PACK - 1 : PACK])
             quantise_x(1, q)
+            if q == 0:
+                quantise_x(0, 1, "x_bf10")
             scores(q)

from contextlib import ExitStack

import concourse.mybir as mybir

F32 = mybir.dt.float32
BF16 = mybir.dt.bfloat16
I32 = mybir.dt.int32
U32 = mybir.dt.uint32
U16 = mybir.dt.uint16
U8 = mybir.dt.uint8
FP8X4 = mybir.dt.float8_e4m3fn_x4
FP4X4 = mybir.dt.float4_e2m1fn_x4
ACT = mybir.ActivationFunctionType
ALU = mybir.AluOpType

K, K2, T, S, H, N, T2, PICK = 1024, 512, 2048, 512, 1024, 512, 2048, 1024
P = 128
PACK = 4
PASS = P * PACK
QUADS = 4
HALF = PICK // 2
QUARTER = PICK // 4

FLOPS = 2 * (2 * K * H * S + K2 * H * S + 2 * H * N * PICK)


def tile_list_roast_profile_shelf_kernel(
    tc, tab_words, tab_scales, tab2_words, tab2_scales, offs, offs2, offs3, offs4, offs5,
    wa_words, wa_scales, wb, wc_words, wc_scales, gc, page0, wg1, wg2, gx, w4, w5_words, w5_scales, out,
):
    nc = tc.nc
    with ExitStack() as ctx:
        keep = ctx.enter_context(tc.tile_pool(name="keep", bufs=1))
        ring = ctx.enter_context(tc.tile_pool(name="ring", bufs=2))
        psum = ctx.enter_context(tc.psum_pool(name="psum", bufs=1))

        def bank(i):
            return psum.tile([P, 512], F32, name=f"bank{i}", tag=f"bank{i}")

        def load_list(src, name):
            tile = keep.tile([P, src.shape[1]], U16, name=name)
            nc.sync.dma_start(tile[:], src)
            return tile

        def load_table_words(src, name, tag):
            tile = keep.tile([P, T], I32, name=name, tag=tag, align_bytes=64)
            nc.sync.dma_start(tile[:], src.rearrange("p t i -> p (t i)").bitcast(I32))
            return tile

        def zeroed(engine, width, name, tag=None):
            tile = keep.tile([P, width], U8, name=name, tag=tag or name, align_bytes=64)
            engine.memset(tile[:].bitcast(I32), 0)
            return tile

        def load_plane(queue, tile, src):
            passes = src.shape[0]
            for q in range(QUADS):
                queue.dma_start(
                    tile[32 * q : 32 * q + 4, :].bitcast(I32).rearrange("r (a c) -> r a c", a=passes),
                    src[:, 4 * q : 4 * q + 4, :].bitcast(I32).rearrange("a r c -> r a c"),
                )

        def load_dealt_gain(queue, tile, src, t0, t1):
            rows = src.rearrange("(q t) s -> q t s", t=PACK)
            for q in (0, 2, 1, 3):
                queue.dma_start(tile[32 * q : 32 * q + 32, :, :], rows[:, t0:t1, :])

        page_rows = page0.rearrange("(b p t) c -> b t p c", p=P, t=PACK)
        table_tag = ("wa_plane_raw", "wb_raw1")
        pages, page_tag = {}, {}

        def load_page(b, t, tag=None):
            page_tag[b, t] = tag or f"page{b}{t}"
            pages[b, t] = keep.tile([P, T2], F32, name=f"page{b}{t}", tag=page_tag[b, t], align_bytes=64)
            nc.sync.dma_start(pages[b, t][:], page_rows[b, t])

        def load_float_weight(src, name, tag):
            tile = keep.tile([P, PACK, 512], F32, name=name, tag=tag, align_bytes=64)
            nc.sync.dma_start(tile[:], src.rearrange("(p i) c -> p i c", i=PACK))
            return tile

        def quantise(src, name, tag, codes_tag=None):
            width = src.shape[1] // PACK
            codes = keep.tile([P, width], U32, name=name + "_codes", tag=codes_tag or tag + "_codes", align_bytes=64)
            scales = keep.tile([P, width], U8, name=name + "_scales", tag=tag + "_scales", align_bytes=64)
            nc.vector.quantize_mx(out=codes[:].bitcast(FP8X4), scales=scales[:], in_=src)
            return codes, scales

        def load_plane_filled(tile, src):
            for q in range(QUADS):
                nc.sync.dma_start(
                    tile[32 * q : 32 * q + 32, :].bitcast(I32),
                    src[4 * q : 4 * q + 4, :].bitcast(I32).partition_broadcast(8),
                )

        def load_two_planes(tile, src):
            for q in range(QUADS):
                nc.sync.dma_start(tile[32 * q : 32 * q + 8, :].bitcast(I32), src[:, 4 * q : 4 * q + 4, :].bitcast(I32))

        def move_second_plane(dst, src):
            for q in range(QUADS):
                nc.sync.dma_start(dst[32 * q : 32 * q + 4, :].bitcast(I32), src[32 * q + 4 : 32 * q + 8, :].bitcast(I32))

        t_plane = zeroed(nc.vector, T, "t_plane")
        wa_plane_raw = zeroed(nc.vector, H, "wa_plane_raw")
        v_plane1 = zeroed(nc.vector, S, "v_plane1")
        wa_plane1 = zeroed(nc.vector, H, "wa_plane1")

        idx2 = load_list(offs2, "idx2")
        t2_plane = keep.tile([P, T], U8, name="t2_plane", tag="t2_plane", align_bytes=64)
        load_plane_filled(t2_plane, tab2_scales[0])
        t2_words = load_table_words(tab2_words[0], "t2_words", "t2_words")
        wc_raw = keep.tile([P, H], I32, name="wc_raw", tag="wc_raw", align_bytes=64)
        nc.sync.dma_start(wc_raw[:], wc_words[0].rearrange("p c i -> p (c i)").bitcast(I32))
        wc_plane_raw = keep.tile([P, H], U8, name="wc_plane_raw", tag="wc_plane_raw", align_bytes=64)
        load_plane_filled(wc_plane_raw, wc_scales[0])
        gc_col = keep.tile([P, 2, PACK], F32, name="gc_col")
        nc.sync.dma_start(gc_col[:], gc.rearrange("(b p t) -> p b t", p=P, t=PACK))
        load_page(0, 0)
        idx4 = load_list(offs4, "idx4")
        wg2_first = keep.tile([P, 1, S], F32, name="wg2_first", tag="wg2_first", align_bytes=64)
        load_dealt_gain(nc.sync, wg2_first, wg2, 0, 1)
        load_page(1, 0)
        wg2_second = keep.tile([P, 1, S], F32, name="wg2_second")
        load_dealt_gain(nc.sync, wg2_second, wg2, 1, 2)
        load_page(0, 1)
        idx = load_list(offs, "idx")
        load_page(1, 1)
        wg2_rest = keep.tile([P, 2, S], F32, name="wg2_rest", tag="wg2_rest", align_bytes=64)
        load_dealt_gain(nc.sync, wg2_rest, wg2, 2, PACK)
        v_planes = keep.tile([P, S], U8, name="v_planes", align_bytes=64)
        wa_planes = keep.tile([P, H], U8, name="wa_planes", align_bytes=64)
        v_scales = (v_planes, v_plane1)
        wa_scale = (wa_planes, wa_plane1)
        wb_raw = {}

        def load_wb(a, b):
            wb_raw[a, b] = load_float_weight(wb[PASS * a : PASS * (a + 1), 512 * b : 512 * (b + 1)], f"wb_raw{a}{b}", (f"wb_raw{a}", ("wb_raw1", "bf10")[a])[b])

        load_page(0, 2)
        load_two_planes(wa_plane_raw, wa_scales)
        load_wb(0, 0)
        load_two_planes(t_plane, tab_scales)
        load_page(1, 2)
        idx3 = load_list(offs3, "idx3")
        idx5 = load_list(offs5, "idx5")
        load_wb(1, 0)
        gx_col = keep.tile([P, 2, PACK], F32, name="gx_col")
        nc.sync.dma_start(gx_col[:], gx.rearrange("(b p t) -> p b t", p=P, t=PACK))
        t_words = [load_table_words(tab_words[0], "t_words0", "t_words0")]
        wa_raw = keep.tile([P, H], I32, name="wa_raw", align_bytes=64)
        nc.sync.dma_start(
            wa_raw[:].rearrange("p (a c) -> p a c", a=2), wa_words.bitcast(I32).rearrange("a p c -> p a c")
        )
        load_page(0, 3, "t2_words")

        v2_plane = keep.tile([P, S], U8, name="v2_plane", align_bytes=64)
        nc.vector.tensor_copy(v2_plane[:], t2_plane[:].indirect(idx2[:]))
        v2_codes = keep.tile([P, S], U32, name="v2_codes", tag="v2_codes", align_bytes=64)
        nc.vector.tensor_copy(v2_codes[:], t2_words[:].bitcast(U32).indirect(idx2[:]))
        wc_plane = keep.tile([P, H], U8, name="wc_plane", tag="wc_plane", align_bytes=64)
        wc_codes = keep.tile([P, H], U32, name="wc_codes", align_bytes=64)
        for b in range(2):
            for t0, t1 in ((0, 1), (1, PACK)):
                nc.vector.tensor_copy(
                    wc_plane[:, 512 * b : 512 * (b + 1)].rearrange("p (t m) -> p t m", t=PACK)[:, t0:t1, :],
                    wc_plane_raw[:, 512 * b : 512 * (b + 1)].rearrange("p (m t) -> p t m", t=PACK)[:, t0:t1, :],
                )
            nc.scalar.copy(
                wc_codes[:, 512 * b : 512 * (b + 1)].rearrange("p (t m) -> p m t", t=PACK),
                wc_raw[:, 512 * b : 512 * (b + 1)].bitcast(U32).rearrange("p (m t) -> p m t", t=PACK),
            )

        def curve(b, t):
            cols = slice(512 * b + P * t, 512 * b + P * (t + 1))
            c = bank(0)
            nc.tensor.matmul_mx(
                out=c[:], lhsT=wc_codes[:, cols].bitcast(FP8X4), lhsT_scale=wc_plane[:, cols],
                rhs=v2_codes[:].bitcast(FP8X4), rhs_scale=v2_plane[:], start=True, stop=True,
            )
            feature = ring.tile([P, S], F32, name="feature", tag="result", bufs=8)
            halves = (slice(0, S // 2), slice(S // 2, S))
            for h in halves:
                nc.scalar.activation(feature[:, h], c[:, h], ACT.Abs)
            for h in halves:
                nc.scalar.activation(feature[:, h], feature[:, h], ACT.Exp, scale=-1.0)
            for h in halves:
                nc.scalar.activation(feature[:, h], feature[:, h], ACT.Copy, scale=gc_col[:, b, t : t + 1])
            gain = (wg2_first[:, 0, :], wg2_second[:, 0, :], wg2_rest[:, 0, :], wg2_rest[:, 1, :])[t]
            nc.vector.tensor_tensor(pages[b, t][:].indirect(idx4[:]), feature[:], gain, ALU.mult)

        def round_wb(raw, name, tag):
            rounded = keep.tile([P, 512 * PACK], BF16, name=name, tag=tag, align_bytes=64)
            nc.scalar.copy(
                rounded[:].rearrange("p (t m i) -> p m t i", t=PACK, i=PACK),
                raw[:].rearrange("p i (m t) -> p m t i", t=PACK),
            )
            return rounded

        def round_w4(raw, name, tag):
            rounded = keep.tile([P, 512 * PACK], BF16, name=name, tag=tag, align_bytes=64)
            nc.scalar.copy(rounded[:].rearrange("p (c i) -> p c i", i=PACK), raw[:].rearrange("p i c -> p c i"))
            return rounded

        wb_q, w4_bf, w4_q, v_codes = {}, {}, {}, {}

        def prepare_wb(a, b):
            wb_q[a, b] = quantise(round_wb(wb_raw[a, b], f"wb_bf{a}{b}", f"bf{a}{b}")[:], f"wb{a}{b}", f"wb{a}{b}")

        def prepare_w4(b):
            raw = load_float_weight(w4[PASS * b : PASS * (b + 1), :], f"w4_raw{b}", table_tag[b])
            w4_bf[b] = round_w4(raw, f"w4_bf{b}", ("bf00", "wc_raw")[b])

        def gather_v(a):
            v_codes[a] = keep.tile([P, S], U32, name=f"v_codes{a}", align_bytes=64)
            nc.vector.tensor_copy(v_codes[a][:], t_words[a][:].bitcast(U32).indirect(idx[:]))

        curve(0, 0)
        curve(1, 0)
        curve(0, 1)
        curve(1, 1)
        curve(0, 2)
        nc.vector.tensor_copy(v_planes[:], t_plane[:].indirect(idx[:]))
        nc.vector.tensor_copy(
            wa_planes[:].rearrange("p (b t m) -> p b t m", b=2, t=PACK),
            wa_plane_raw[:].rearrange("p (b m t) -> p b t m", b=2, t=PACK),
        )
        t_words.append(load_table_words(tab_words[1], "t_words1", "wa_plane_raw"))
        load_page(1, 3, "t_plane")
        move_second_plane(wa_plane1, wa_planes)
        move_second_plane(v_plane1, v_planes)
        prepare_wb(0, 0)
        wg1_first = keep.tile([P, 2, S], F32, name="wg1_first", tag="wb_raw0", align_bytes=64)
        load_dealt_gain(nc.sync, wg1_first, wg1, 0, 2)
        curve(1, 2)
        prepare_wb(1, 0)
        wa_codes = keep.tile([P, 2 * H], U16, name="wa_codes", align_bytes=64)
        nc.scalar.copy(
            wa_codes[:].rearrange("p (g t m) -> p g t m", g=4, t=PACK),
            wa_raw[:].bitcast(U16).rearrange("p (g m t) -> p g t m", g=4, t=PACK),
        )
        for a in range(2):
            gather_v(a)
            load_wb(a, 1)
        wg1_rest = keep.tile([P, 2, S], F32, name="wg1_rest", tag="t_words0", align_bytes=64)
        load_dealt_gain(nc.sync, wg1_rest, wg1, 2, PACK)
        curve(0, 3)
        curve(1, 3)
        order = [(b, t) for b in range(2) for t in range(PACK)]
        lower = {}
        for b, t in order:
            pa = bank(4 + t % 2)
            for a in (1, 0):
                cols = slice(H * a + 512 * b + P * t, H * a + 512 * b + P * (t + 1))
                nc.tensor.matmul_mx(
                    out=pa[:], lhsT=wa_codes[:, cols].bitcast(FP4X4), lhsT_scale=wa_scale[a][:, 512 * b + P * t : 512 * b + P * (t + 1)],
                    rhs=v_codes[a][:].bitcast(FP8X4), rhs_scale=v_scales[a][:], start=a == 1, stop=a == 0,
                )
            if (b, t) == order[-1]:
                lower[b, t] = keep.tile([P, S], F32, name="lower", tag="x00_codes", align_bytes=64)
            else:
                lower[b, t] = ring.tile([P, S], F32, name="lower", tag="result", bufs=8)
            nc.scalar.copy(lower[b, t][:], pa[:])
        for a in range(2):
            prepare_wb(a, 1)

        x_rows, x_bf, x_q = {}, {}, {}

        def bean_features(b, t):
            pb = bank(6 + t % 2)
            cols = slice(P * t, P * (t + 1))
            for a in range(2):
                codes, scales = wb_q[a, b]
                nc.tensor.matmul_mx(
                    out=pb[:], lhsT=codes[:, cols].bitcast(FP8X4), lhsT_scale=scales[:, cols],
                    rhs=v_codes[a][:].bitcast(FP8X4), rhs_scale=v_scales[a][:], start=a == 0, stop=a == 1,
                )
            u = PACK * b + t
            first = lower[b, t]
            if u >= 2:
                done = order[u - 1 if u + 1 == len(order) else u - 2]
                lower[b, t] = keep.tile([P, S], F32, name="h1", tag=page_tag[done], align_bytes=64)
            nc.vector.tensor_tensor(lower[b, t][:], pb[:], first[:], ALU.min)

        def put_bean(b, t):
            gain = (wg1_first, wg1_rest)[t // 2][:, t % 2, :]
            nc.vector.tensor_tensor(pages[b, t][:].indirect(idx3[:]), lower[b, t][:], gain, ALU.mult)

        x_width = (HALF, QUARTER)

        def pick(b, t, j0, j1):
            if j0 == PICK - QUARTER:
                picked = keep.tile([P, j1 - j0], F32, name="picked", tag="x_bf11", align_bytes=64)
            else:
                picked = ring.tile([P, j1 - j0], F32, name="picked", tag="picked", bufs=3)
            nc.vector.tensor_copy(picked[:], pages[b, t][:].indirect(idx5[:, j0 // 16 : j1 // 16]))
            return picked

        def fetch(b, t):
            w = x_width[b]
            picked = pick(b, t, 0, PICK)
            for h in range(PICK // w):
                if t == 0:
                    tag = table_tag[h] if b == 0 else f"x_rows{h}"
                    x_rows[b, h] = keep.tile([P, PACK - b, w], BF16, name=f"x_rows{b}{h}", tag=tag, align_bytes=64)
                nc.scalar.activation(
                    x_rows[b, h][:, t, :], picked[:, w * h : w * (h + 1)], ACT.Copy, scale=gx_col[:, b, t : t + 1]
                )

        def weave(b, h):
            x_bf[b, h] = keep.tile([P, x_width[b], PACK], BF16, name=f"x_bf{b}{h}", tag=f"x_bf{b}{h}", align_bytes=64)
            nc.scalar.copy(
                x_bf[b, h][:, :, 0 : PACK - b].rearrange("p (c e) t -> p c t e", e=PACK),
                x_rows[b, h][:].rearrange("p t (c e) -> p c t e", e=PACK),
            )

        def quantise_x(b, h, codes_tag=None):
            x_q[b, h] = quantise(x_bf[b, h][:].rearrange("p c t -> p (c t)"), f"x{b}{h}", f"x{b}{h}", codes_tag)

        w5_codes = keep.tile([P, 2 * N], U16, name="w5_codes", tag="wg2_rest", align_bytes=64)

        def w4_part(b, n):
            codes, scales = w4_q[b]
            return codes[:, P * n : P * (n + 1)].bitcast(FP8X4), scales[:, P * n : P * (n + 1)]

        def w5_part(b, n):
            cols = slice(N * b + P * n, N * b + P * (n + 1))
            return w5_codes[:, cols].bitcast(FP4X4), w5_plane[:, cols]

        def scores(q):
            for g in range(2):
                y1, y2 = bank(4 * (q % 2) + 2 * g), bank(4 * (q % 2) + 2 * g + 1)
                for y, weight in ((y2, w5_part), (y1, w4_part)):
                    for b in range(2):
                        h, j = divmod(QUARTER * q, x_width[b])
                        codes, scales = x_q[b, h]
                        for i in range(2):
                            lhsT, lhsT_scale = weight(b, 2 * g + i)
                            nc.tensor.matmul_mx(
                                out=y[:, QUARTER * i : QUARTER * (i + 1)], lhsT=lhsT, lhsT_scale=lhsT_scale,
                                rhs=codes[:, j : j + QUARTER].bitcast(FP8X4), rhs_scale=scales[:, j : j + QUARTER],
                                start=b + i == 0, stop=b + i == 2,
                            )
                second = ring.tile([P, HALF], F32, name="second", tag="staged", bufs=4)
                nc.scalar.copy(second[:], y2[:])
                larger = ring.tile([P, HALF], F32, name="larger", tag="result", bufs=8)
                nc.vector.tensor_tensor(larger[:], y1[:], second[:], ALU.max)
                nc.sync.dma_start(
                    out[2 * P * g : 2 * P * (g + 1), QUARTER * q : QUARTER * (q + 1)].rearrange("(i p) c -> p i c", p=P),
                    larger[:].rearrange("p (i c) -> p i c", i=2),
                )

        w5_plane = zeroed(nc.vector, 2 * N, "w5_plane", "bf11")
        load_plane(nc.sync, w5_plane, w5_scales)
        prepare_w4(0)
        prepare_w4(1)
        nc.sync.dma_start(
            w5_codes[:].bitcast(I32).rearrange("p (a c) -> p a c", a=2),
            w5_words.bitcast(I32).rearrange("a p c -> p a c"),
        )
        bean_features(0, 0)
        for u, (b, t) in enumerate(order):
            put_bean(b, t)
            if u + 2 < len(order):
                bean_features(*order[u + 1])
            if u + 1 < len(order):
                fetch(b, t)
            if u + 1 == PACK:
                for h in range(2):
                    weave(0, h)
            if u + 2 == len(order):
                bean_features(*order[u + 1])
                for a in range(2):
                    w4_q[a] = quantise(w4_bf[a][:], f"w4{a}", f"wb{a}1")
                quantise_x(0, 0)
                for q in range(PICK // QUARTER):
                    weave(1, q)
        for q in range(PICK // QUARTER):
            picked = pick(1, PACK - 1, QUARTER * q, QUARTER * (q + 1))
            nc.scalar.activation(x_bf[1, q][:, :, PACK - 1], picked[:], ACT.Copy, scale=gx_col[:, 1, PACK - 1 : PACK])
            quantise_x(1, q)
            if q == 0:
                quantise_x(0, 1, "x_bf10")
            scores(q)
